import numpy as np
import ml_dtypes


def mxq(x, axis, fmt="e4m3"):
    dtype, down = {"e4m3": (ml_dtypes.float8_e4m3fn, 7), "e5m2": (ml_dtypes.float8_e5m2, 14)}[fmt]
    v = np.moveaxis(np.asarray(x, np.float32).astype(ml_dtypes.bfloat16).astype(np.float64), axis, -1)
    blocks = v.reshape(v.shape[:-1] + (-1, 32))
    amax = np.abs(blocks).max(-1, keepdims=True)
    byte = np.maximum(np.where(amax > 0, np.frexp(amax)[1] - 1 + 127, 0) - down, 1)
    scale = np.exp2(byte - 127.0)
    codes = (blocks / scale).astype(np.float32).astype(dtype).astype(np.float64)
    return np.moveaxis((codes * scale).reshape(v.shape), -1, axis)


WIDE = False


def mx_kscale(k):
    if not WIDE:
        return np.ones(k)
    levels = np.array([10, -10, 5, -5, 0])
    if k % 512:
        return np.exp2(np.random.permutation(np.resize(levels, k // 32))).repeat(32)
    a = np.empty((k // 512, 16))
    for p in range(k // 512):
        a[p, :8] = np.random.permutation(np.resize(levels, 8))
        for g in range(8):
            far = levels[np.abs(levels - a[p, g]) >= 10]
            a[p, g + 8] = far[np.random.randint(len(far))]
    return np.exp2(a.ravel()).repeat(32)


BF16 = ml_dtypes.bfloat16


def bf(x):
    return np.asarray(x, np.float32).astype(BF16)


def f64(x):
    return np.asarray(x).astype(np.float64)


E2M1 = np.array([0.0, 0.5, 1.0, 1.5, 2.0, 3.0, 4.0, 6.0, -0.0, -0.5, -1.0, -1.5, -2.0, -3.0, -4.0, -6.0])


def pack_weight(w, fmt):
    k, n = w.shape
    w = f64(bf(w)).reshape(k // 32, 32, n)
    amax = np.abs(w).max(1)
    if fmt == "e4m3":
        byte = np.frexp(amax)[1] - 1 + 127 - 7
    else:
        mant, ex = np.frexp(amax / 6.0)
        byte = np.where(mant > 0.5, ex, ex - 1) + 127
    byte = np.clip(np.where(amax > 0, byte, 1), 1, 254)
    scaled = (w * np.exp2(127.0 - byte)[:, None, :]).reshape(k, n).astype(np.float32)
    by_word = np.ascontiguousarray(scaled.reshape(k // 512, 128, 4, n).transpose(0, 1, 3, 2))
    if fmt == "e4m3":
        words = by_word.astype(ml_dtypes.float8_e4m3fn).view(np.uint8)
    else:
        c = by_word.astype(ml_dtypes.float4_e2m1fn).view(np.uint8) & 0xF
        words = c[..., 0::2] | (c[..., 1::2] << 4)
    return np.ascontiguousarray(words), np.ascontiguousarray(byte.astype(np.uint8).reshape(k // 512, 16, n))


def unpack_weight(words, scales, fmt):
    g, p, n, _ = words.shape
    if fmt == "e4m3":
        vals = np.ascontiguousarray(words).view(ml_dtypes.float8_e4m3fn).astype(np.float64)
    else:
        nib = np.empty((g, p, n, 4), np.uint8)
        nib[..., 0::2] = words & 0xF
        nib[..., 1::2] = words >> 4
        vals = E2M1[nib]
    vals = vals * np.repeat(np.exp2(scales.astype(np.float64) - 127.0), 8, axis=1)[..., None]
    return vals.transpose(0, 1, 3, 2).reshape(g * 512, n)

E4M3FN = np.array([(-1.0 if i & 128 else 1.0) * ((1.0 + (i & 7) / 8.0) * 2.0 ** (((i >> 3) & 15) - 7) if i & 120 else (i & 7) * 2.0 ** -9) for i in range(256)])


def e4m3fn_bytes(y):
    return np.clip(np.asarray(y, np.float64), -448.0, 448.0).astype(np.float32).astype(ml_dtypes.float8_e4m3fn).view(np.uint8)


def e4m3fn_values(b):
    return E4M3FN[b]


S, F, N, P, R = 1024, 512, 1024, 1024, 5

CUTS = (-1.5, -0.5, 0.5, 1.5)


def sigmoid(v):
    return 1.0 / (1.0 + np.exp(-v))


def cumulative_probs(theta, y):
    return [sigmoid(theta[None, :] + c - y) for c in CUTS]


def state_probs(q):
    p = [q[0]]
    for r in range(1, len(q)):
        p.append(q[r] - q[r - 1])
    p.append(1.0 - q[-1])
    return p


def draw0():
    s, t = mx_kscale(F), mx_kscale(N)
    z = bf(np.random.standard_normal((S, F)) * s)
    load_words, load_scales = pack_weight(np.random.standard_normal((F, N)) * (2.0 / np.sqrt(F)) / s[:, None], "e4m3")
    return {"z": z,
            "load_words": load_words,
            "load_scales": load_scales,
            "theta": bf(np.random.standard_normal(N) * 0.5),
            "val": bf(np.random.standard_normal((R, N)) * t[None, :]),
            "expo": bf(np.random.standard_normal((N, P)) / np.sqrt(N) / t[:, None])}


def core(z, load_words, load_scales, theta, val, expo):
    theta, val = f64(theta), f64(val)
    y = mxq(f64(z), 1, "e4m3") @ unpack_weight(load_words, load_scales, "e4m3")
    q = cumulative_probs(theta, y)
    p = state_probs(q)
    u = p[0] * val[0][None, :]
    for r in range(1, val.shape[0]):
        u = u + p[r] * val[r][None, :]
    return mxq(u, 1, "e4m3") @ mxq(f64(expo), 0, "e4m3")


def setup_inputs():
    drawn = draw0()
    full = np.asarray(drawn['expo']).astype(np.float64)
    scale = (np.abs(full).reshape(1024, 8, 128).max(axis=(2,)) / 448.0).astype(np.float32)
    given = {}
    for key, value in drawn.items():
        if key == 'expo':
            given['expo_bytes'] = e4m3fn_bytes(full / np.repeat(scale.astype(np.float64), 128, axis=1))
            given['expo_scale'] = scale
        else:
            given[key] = value
    return given


def reference(z, load_words, load_scales, theta, val, expo_bytes, expo_scale):
    return core(z, load_words, load_scales, theta, val, e4m3fn_values(expo_bytes) * np.repeat(expo_scale.astype(np.float64), 128, axis=1))

from contextlib import ExitStack

import concourse.mybir as mybir
from concourse.masks import make_identity

S, F, N, P, R = 1024, 512, 1024, 1024, 5
CUTS = (-1.5, -0.5, 0.5, 1.5)
FLOPS = 2 * S * F * N + 2 * S * N * P

F32 = mybir.dt.float32
BF16 = mybir.dt.bfloat16
I32 = mybir.dt.int32
U32 = mybir.dt.uint32
U8 = mybir.dt.uint8
FP8 = mybir.dt.float8_e4m3fn
FP8X4 = mybir.dt.float8_e4m3fn_x4
ALU = mybir.AluOpType
ACT = mybir.ActivationFunctionType

Q_BUFS = 11
CHUNKS = ((0, 256), (256, 512), (768, 256))
DOUBLE = (8, 9, 10)
NDOUBLE = 3
DLO = 8
DHI = 16
BANKS = {"y": 2, "x": 4, "o": 2}
X_LEAD = 1
EXPO_ENGINE = "VSVVVVVVSVSSVSVS"
S_WHEN = (0, 3, 6, 9, 10, 10)
Z_ENG = ("VV", "V", "S")
PZ_AT = (0, 1, 1)
VZ_AT = (0, 0, 6)
MM2 = ((12, 14, 18, 19), (21, 22, 23, 23, 23, 23, 23, 23))
V_FIRST = 1
V_SECOND = 4
V_FILL0 = 10
V_FILL = (0, 1, 2, 4, 12, 3, 15, 8, 14, 16, 4, 1)


def tile_orderedlogitratingmigrationportfoliovalu_d1p_kernel(
    tc, z, load_words, load_scales, theta, val, expo_bytes, expo_scale, out
):
    nc = tc.nc
    with ExitStack() as ctx:
        keep = ctx.enter_context(tc.tile_pool(name="keep", bufs=1))
        work = ctx.enter_context(tc.tile_pool(name="work", bufs=2))
        psum = ctx.enter_context(tc.psum_pool(name="psum", bufs=4))
        ctx.enter_context(tc.manual_schedule())

        def kept(name, shape, dtype):
            return keep.tile(shape, dtype, name=name, tag=name, align_bytes=64)

        ident = kept("ident", [128, 128], F32)
        dummy = kept("dummy", [128, 2], F32)
        vt = kept("vt", [128, 512], BF16)
        spl = kept("spl", [128, 1024], U8)
        sp = kept("sp", [128, 1024], U8)
        wl = kept("wl", [128, 1024], I32)
        wp = kept("wp", [128, 1024], I32)
        vg = kept("vg", [128, 48], BF16)
        bias = kept("bias", [128, 32], F32)
        dd = kept("dd", [128, 32], F32)
        v4 = kept("v4", [128, 8], F32)
        v4b = kept("v4b", [128, 1024], F32)
        dg = [kept("dg%d" % n, [128, 128], F32) for n in range(8)]
        all_units = [(c, g, t) for c in range(len(CHUNKS)) for g in range(2) for t in range(4)]
        dg1 = {}
        for k in DOUBLE:
            n = 4 * all_units[k][1] + all_units[k][2]
            if n not in dg1:
                dg1[n] = kept("dh%d" % n, [128, 128], F32)
        es = kept("es", [128, 2, 4, 8], F32)
        eb = [kept("eb%d" % g, [128, 4, 1024], U8) for g in range(2)]
        ec = [kept("ec%d" % e, [128, 512], U32) for e in range(4)]
        ecs = [kept("ecs%d" % e, [128, 512], U8) for e in range(4)]
        wb = [kept("wb%d" % e, [128, 4, 512], BF16) for e in range(4)]
        zt = [kept("zt%d" % c, [128, w // 128, F], BF16) for c, (s0, w) in enumerate(CHUNKS)]
        zg = [kept("zg%d" % c, [128, 4 * w], BF16) for c, (s0, w) in enumerate(CHUNKS)]
        zc = [kept("zc%d" % c, [128, w], U32) for c, (s0, w) in enumerate(CHUNKS)]
        zs = [kept("zs%d" % c, [128, w], U8) for c, (s0, w) in enumerate(CHUNKS)]
        uc = {}
        us = {}
        for c, (s0, w) in enumerate(CHUNKS):
            for g in range(2):
                uc[c, g] = kept("uc%d%d" % (c, g), [128, w], U32)
                us[c, g] = kept("us%d%d" % (c, g), [128, w], U8)

        nc.vector.memset(dummy[:], 0.0)
        nc.vector.memset(vt[:].bitcast(I32), 0)
        nc.vector.memset(spl[:].bitcast(I32), 0)
        nc.scalar.activation(dummy[:, 1:2], dummy[:, 0:1], ACT.Sigmoid)

        def load_z(c):
            s0, w = CHUNKS[c]
            nc.sync.dma_start(out=zt[c][:], in_=z[s0 : s0 + w, :].rearrange("(p j) k -> p j k", p=128))

        def load_w(g):
            cols = slice(512 * g, 512 * (g + 1))
            src = load_words[0].rearrange("p n t -> p (n t)")[:, 2048 * g : 2048 * (g + 1)]
            nc.sync.dma_start(out=wl[:, cols], in_=src.bitcast(I32))

        def load_e(g, t0, t1):
            src = expo_bytes.rearrange("(g p t) n -> g p t n", p=128, t=4)[g]
            nc.sync.dma_start(out=eb[g][:, t0:t1, :], in_=src[:, t0:t1, :])

        nc.sync.dma_start(out=es[:], in_=expo_scale.rearrange("(g p t) j -> p g t j", p=128, t=4))
        load_e(0, 0, 2)
        load_z(0)
        nc.gpsimd.dma_start(out=vt[0:10, :], in_=val.rearrange("r (g k) -> (r g) k", g=2))
        nc.gpsimd.dma_start(out=vt[10:12, :], in_=theta.rearrange("(g k) -> g k", g=2))
        make_identity(nc, ident[:])
        for q in range(4):
            nc.scalar.dma_start(
                out=spl[32 * q : 32 * q + 4, :].bitcast(I32), in_=load_scales[0, 4 * q : 4 * q + 4, :].bitcast(I32)
            )
        load_w(0)
        load_e(0, 2, 4)
        load_z(1)
        load_w(1)
        load_e(1, 0, 4)
        load_z(2)

        lists = {"P": [], "S": [], "V": [], "G": []}

        def op(engine, needs, gives, fn):
            lists[engine].append((needs, gives, fn))

        bank_count = {"y": 0, "o": 0, "x": 0}
        bank_free = {"y": [], "o": [], "x": []}
        bufs = BANKS

        def bank_need(tag, free_key):
            n = bank_count[tag]
            bank_count[tag] = n + 1
            bank_free[tag].append(free_key)
            return [bank_free[tag][n - bufs[tag]]] if n >= bufs[tag] else []

        def psum_tile(tag):
            return psum.tile([128, 512], F32, name=tag, tag=tag, bufs=bufs[tag])

        tiles = {}

        def params_turn():
            pv = psum_tile("o")
            tiles["pv"] = pv
            vwords = vt[:].bitcast(F32)
            for u in range(2):
                nc.tensor.transpose(pv[:, 128 * u : 128 * (u + 1)], vwords[:, u:256:2], ident[:])

        def params_copy():
            nc.vector.tensor_copy(
                out=vg[:].bitcast(F32).rearrange("p (r u) -> p r u", u=2),
                in_=tiles["pv"][:, 0:256].rearrange("p (u r) -> p r u", u=2)[:, 0:12, :],
            )

        def params_bias():
            for r in range(4):
                nc.vector.tensor_scalar(bias[:, 8 * r : 8 * r + 8], vg[:, 40:48], CUTS[r], None, ALU.add)

        def params_d():
            nc.vector.tensor_sub(dd[:], vg[:, 0:32], vg[:, 8:40])
            nc.vector.tensor_copy(out=v4[:], in_=vg[:, 32:40])

        def make_diag():
            for n in range(8):
                nc.gpsimd.tensor_scalar(dg[n][:], ident[:], dd[:, n : n + 1], 0.0, ALU.mult, ALU.add)
            for n in dg1:
                nc.gpsimd.tensor_scalar(dg1[n][:], ident[:], dd[:, 8 + n : 9 + n], 0.0, ALU.mult, ALU.add)

        def spread_turn(b):
            bank = psum_tile("o")
            tiles["spread", b] = bank
            for i in range(4):
                n = 4 * b + i
                nc.tensor.transpose(
                    bank[:, 128 * i : 128 * (i + 1)], v4[:, n : n + 1].to_broadcast([128, 128]), ident[:]
                )

        def spread_copy(b, engine):
            if engine == "V":
                nc.vector.tensor_copy(out=v4b[:, 512 * b : 512 * (b + 1)], in_=tiles["spread", b][:])
            else:
                nc.scalar.copy(out=v4b[:, 512 * b : 512 * (b + 1)], in_=tiles["spread", b][:])

        def prefill(k):
            c, g, t = units[k]
            n = 4 * g + t
            bank = psum_tile("x")
            tiles["x", k] = bank
            for j in range(CHUNKS[c][1] // 128):
                nc.tensor.matmul(
                    bank[:, 128 * j : 128 * (j + 1)],
                    lhsT=v4b[:, 128 * n : 128 * (n + 1)],
                    rhs=ident[:],
                    is_transpose=True,
                    start=(j == 0),
                    stop=False,
                )

        def diag(k):
            c, g, t = units[k]
            w = CHUNKS[c][1]
            n = 4 * g + t
            nc.tensor.matmul(
                tiles["x", k][:, 0:w], lhsT=dg[n][:], rhs=tiles["q", k, 0][:, 0:w], start=False, stop=k not in DOUBLE
            )
            if k in DOUBLE:
                nc.tensor.matmul(
                    tiles["x", k][:, 0:w], lhsT=dg1[n][:], rhs=tiles["q", k, 1][:, 0:w], start=False, stop=True
                )

        def permute(dst, src, g):
            cols = slice(512 * g, 512 * (g + 1))
            nc.vector.tensor_copy(
                out=dst[:, cols].rearrange("p (t m) -> p t m", t=4), in_=src[:, cols].rearrange("p (m t) -> p t m", t=4)
            )

        def z_turn(c, j):
            bank = psum_tile("o")
            tiles["z", c, j] = bank
            words = zt[c][:, j, :].bitcast(F32)
            for u in range(2):
                nc.tensor.transpose(bank[:, 128 * u : 128 * (u + 1)], words[:, u:256:2], ident[:])

        def z_copy(c, j, engine):
            o = zg[c][:].bitcast(F32)[:, 256 * j : 256 * (j + 1)].rearrange("p (r u) -> p r u", u=2)
            i = tiles["z", c, j][:, 0:256].rearrange("p (u r) -> p r u", u=2)
            if engine == "V":
                nc.vector.tensor_copy(out=o, in_=i)
            else:
                nc.scalar.copy(out=o, in_=i)

        def z_quant(c):
            nc.vector.quantize_mx(out=zc[c][:].bitcast(FP8X4), scales=zs[c][:], in_=zg[c][:])

        units = [(c, g, t) for c in range(len(CHUNKS)) for g in range(2) for t in range(4)]

        def mm1(k):
            c, g, t = units[k]
            y = psum_tile("y")
            tiles["y", k] = y
            cols = slice(512 * g + 128 * t, 512 * g + 128 * (t + 1))
            nc.tensor.matmul_mx(
                out=y[:, 0 : CHUNKS[c][1]],
                lhsT=wp[:, cols].bitcast(FP8X4),
                lhsT_scale=sp[:, cols],
                rhs=zc[c][:].bitcast(FP8X4),
                rhs_scale=zs[c][:],
                start=True,
                stop=True,
            )

        def sig(k):
            c, g, t = units[k]
            w = CHUNKS[c][1]
            for r in range(4):
                q = work.tile([128, 512], F32, name="q%d" % r, tag="q%d" % r, bufs=Q_BUFS, align_bytes=64)
                n = 8 * r + 4 * g + t
                nc.scalar.activation(q[:, 0:w], tiles["y", k][:, 0:w], ACT.Sigmoid, bias=bias[:, n : n + 1], scale=-1.0)
                tiles["q", k, r] = q

        def u_tile(c, g):
            tiles["ub", c, g] = work.tile([128, 4, 512], BF16, name="ub", tag="ub", align_bytes=64)
            tiles["ux", c, g] = work.tile([128, 2048], BF16, name="ux", tag="ux", align_bytes=64)

        def fma(k, r):
            c, g, t = units[k]
            w = CHUNKS[c][1]
            n = 4 * g + t
            if t == 0 and r == (2 if k in DOUBLE else 1):
                u_tile(c, g)
            d = dd[:, 8 * r + n : 8 * r + n + 1]
            first = 2 if k in DOUBLE else 1
            acc = tiles["q", k, first][:, 0:w]
            before = tiles["x", k][:, 0:w] if r == first else acc
            o = tiles["ub", c, g][:, t, 0:w] if r == 3 else acc
            nc.vector.scalar_tensor_tensor(o, tiles["q", k, r][:, 0:w], d, before, ALU.mult, ALU.add)

        def u_inter(c, g, a, b):
            nc.vector.tensor_copy(
                out=tiles["ux", c, g][:, 4 * a : 4 * b].rearrange("p (s t) -> p s t", t=4),
                in_=tiles["ub", c, g][:, :, a:b].rearrange("p t s -> p s t"),
            )

        def u_quant(c, g, a, b):
            nc.vector.quantize_mx(
                out=uc[c, g][:, a:b].bitcast(FP8X4), scales=us[c, g][:, a:b], in_=tiles["ux", c, g][:, 4 * a : 4 * b]
            )

        def widen(g, t, h, engine):
            for b in range(4):
                j = 4 * h + b
                i = eb[g][:, t, 128 * j : 128 * (j + 1)].bitcast(FP8)
                o = wb[2 * g + h][:, t, 128 * b : 128 * (b + 1)]
                s = es[:, g, t, j : j + 1]
                if engine == "V":
                    nc.vector.tensor_scalar(o, i, s, None, ALU.mult)
                else:
                    nc.scalar.activation(o, i, ACT.Copy, scale=s)

        def e_inter(e, a, b):
            if a == 0:
                tiles["wx", e] = work.tile([128, 2048], BF16, name="wx", tag="wx", align_bytes=64)
            nc.vector.tensor_copy(
                out=tiles["wx", e][:, 4 * a : 4 * b].rearrange("p (s t) -> p s t", t=4),
                in_=wb[e][:, :, a:b].rearrange("p t s -> p s t"),
            )

        def e_quant(e):
            nc.vector.quantize_mx(out=ec[e][:].bitcast(FP8X4), scales=ecs[e][:], in_=tiles["wx", e][:])

        def mm2(c, j, h, gs, tag):
            for g in gs:
                if g == 0:
                    tiles["o", c, j, h] = psum_tile(tag)
                cols = slice(128 * j, 128 * (j + 1))
                nc.tensor.matmul_mx(
                    out=tiles["o", c, j, h][:],
                    lhsT=uc[c, g][:, cols].bitcast(FP8X4),
                    lhsT_scale=us[c, g][:, cols],
                    rhs=ec[2 * g + h][:].bitcast(FP8X4),
                    rhs_scale=ecs[2 * g + h][:],
                    start=(g == 0),
                    stop=(g == 1),
                )

        def out_copy(c, j, h, engine, store):
            s0, w = CHUNKS[c]
            if ("ot", c, j) not in tiles:
                tiles["ot", c, j] = work.tile([128, 1024], F32, name="ot", tag="ot", bufs=4, align_bytes=64)
            ot = tiles["ot", c, j]
            cols = slice(512 * h, 512 * (h + 1))
            if engine == "V":
                nc.vector.tensor_copy(out=ot[:, cols], in_=tiles["o", c, j, h][:])
            else:
                nc.scalar.copy(out=ot[:, cols], in_=tiles["o", c, j, h][:])
            rows = out[s0 : s0 + w, :].rearrange("(p j) n -> p j n", p=128)[:, j, :]
            if store == "half":
                nc.sync.dma_start(out=rows[:, cols], in_=ot[:, cols])
            elif store == "row":
                nc.sync.dma_start(out=rows, in_=ot[:])

        E_ENG = {}
        for n, (g, t, h) in enumerate([(g, t, h) for g in range(2) for t in range(4) for h in range(2)]):
            E_ENG[g, t, h] = EXPO_ENGINE[n]

        def P_z(c, j):
            op("P", bank_need("o", ("zc", c, j)), ("zt", c, j), lambda: z_turn(c, j))

        def P_mm1(k):
            c = units[k][0]
            op("P", [("zq", c), ("wp", units[k][1])] + bank_need("y", ("sig", k)), ("y", k), lambda: mm1(k))

        def P_pre(k):
            op("P", [("v4b", units[k][1])] + bank_need("x", ("fma", k, 2 if k in DOUBLE else 1)), ("pre", k), lambda: prefill(k))

        def P_diag(k):
            op("P", [("sig", k), ("dg",)], ("diag", k), lambda: diag(k))

        def P_mm2(c, j, h, gs, tag):
            need = [("uq", c, g, j) for g in gs] + [("eq", 2 * g + h) for g in gs]
            if 0 in gs:
                need = need + bank_need(tag, ("oc", c, j, h))
            op("P", need, ("mm2", c, j, h, gs[-1]), lambda: mm2(c, j, h, gs, tag))

        def Z_copy(c, j, engine):
            op(engine, [("zt", c, j)], ("zc", c, j), lambda: z_copy(c, j, engine))

        def V_zq(c):
            op("V", [("zc", c, j) for j in range(CHUNKS[c][1] // 128)], ("zq", c), lambda: z_quant(c))

        def S_sig(k):
            need = [("y", k), ("bias",)]
            if k >= Q_BUFS:
                need.append(("fma", k - Q_BUFS, 3))
            op("S", need, ("sig", k), lambda: sig(k))

        def V_fma(k, r):
            c, g, t = units[k]
            need = [("sig", k), ("diag", k)]
            grp = 2 * c + g
            if t == 0 and r == (2 if k in DOUBLE else 1) and grp >= 2:
                need.append(("uqall", grp - 2))
            op("V", need, ("fma", k, r), lambda: fma(k, r))

        def E_widen(g, t, h):
            e = E_ENG[g, t, h]
            op(e, [], ("w", g, t, h), lambda: widen(g, t, h, e))

        def V_ei(e, a, b):
            need = [("w", e // 2, t, e % 2) for t in range(4)]
            if e >= 2:
                need.append(("eq", e - 2))
            op("V", need, ("ei", e), lambda: e_inter(e, a, b))

        def V_eq(e):
            op("V", [], ("eq", e), lambda: e_quant(e))

        def V_ui(c, g, a, b):
            op("V", [], ("ui",), lambda: u_inter(c, g, a, b))

        def V_uq(c, g, a, b):
            def f():
                u_quant(c, g, a, b)
                for j in range(a // 128, b // 128):
                    done.add(("uq", c, g, j))

            op("V", [], ("uqall", 2 * c + g), f)

        def O_copy(c, j, h, engine, store):
            need = [("mm2", c, j, h, 1)]
            if store == "row":
                need.append(("oc", c, j, 0))
            op(engine, need, ("oc", c, j, h), lambda: out_copy(c, j, h, engine, store))

        done = set()

        n_units = len(units)
        mm2_at = {}
        for c in range(len(CHUNKS) - 1):
            for n, k in enumerate(MM2[c]):
                mm2_at.setdefault(k, []).append((c, n // 2, n % 2))
        egroups = [(g, t, h) for g in range(2) for t in range(4) for h in range(2)]
        s_e = [x for x in egroups if E_ENG[x] == "S"]
        v_e = [x for x in egroups if E_ENG[x] == "V"]
        op("P", bank_need("o", ("vg",)), ("pv",), params_turn)
        def chunk_j(c):
            return range(CHUNKS[c][1] // 128)
        for j in chunk_j(0):
            P_z(0, j)
        for b in range(2):
            op("P", [("dd",)] + bank_need("o", ("v4b", b)), ("spread", b), lambda b=b: spread_turn(b))
        for k in range(2):
            P_mm1(k)
        for c in range(1, len(CHUNKS)):
            if PZ_AT[c] == -1:
                for j in chunk_j(c):
                    P_z(c, j)
        for k in range(X_LEAD):
            P_pre(k)
        for k in range(n_units):
            if k + 2 < n_units:
                P_mm1(k + 2)
            P_diag(k)
            for c in range(1, len(CHUNKS)):
                if k == PZ_AT[c]:
                    for j in chunk_j(c):
                        P_z(c, j)
            for c, j, h in mm2_at.get(k, []):
                P_mm2(c, j, h, (0, 1), "o")
            if k + X_LEAD < n_units:
                P_pre(k + X_LEAD)
        L = len(CHUNKS) - 1
        for j in chunk_j(L):
            for h in range(2):
                P_mm2(L, j, h, (0,), "x")
        for j in chunk_j(L):
            for h in range(2):
                P_mm2(L, j, h, (1,), "x")

        s_before = {}
        def at(k, fn):
            s_before.setdefault(k, []).append(fn)
        for n, x in enumerate(s_e):
            at(S_WHEN[n], lambda x=x: E_widen(*x))
        for c in range(1, len(CHUNKS)):
            if Z_ENG[c] == "S":
                for j in chunk_j(c):
                    at(PZ_AT[c] + 3 + j, lambda c=c, j=j: Z_copy(c, j, "S"))
        for b in range(2):
            at(0, lambda b=b: op("S", [("spread", b)], ("v4b", b), lambda b=b: spread_copy(b, "S")))
        for j in chunk_j(0):
            if Z_ENG[0][j] == "S":
                at(0, lambda j=j: Z_copy(0, j, "S"))
        for k in range(n_units + 2):
            for f in s_before.get(k, []):
                f()
            if k < n_units:
                S_sig(k)
            for c, j, h in mm2_at.get(k - 2, []):
                O_copy(c, j, h, "S", "row" if h else "")

        op("G", [("dd",)], ("dg",), make_diag)

        for x in v_e[:V_FIRST]:
            E_widen(*x)
        op("V", [("pv",)], ("vg",), params_copy)
        op("V", [], ("dd",), params_d)
        op("V", [], ("bias",), params_bias)
        for j in chunk_j(0):
            if Z_ENG[0][j] == "V":
                Z_copy(0, j, "V")
        op("V", [], ("sp", 0), lambda: permute(sp, spl, 0))
        V_zq(0)
        op("V", [], ("wp", 0), lambda: permute(wp, wl, 0))
        fillers = []
        def fill(n):
            for i in range(n):
                if fillers:
                    fillers.pop(0)()
        fillers.append(lambda: op("V", [], ("sp", 1), lambda: permute(sp, spl, 1)))
        for x in v_e[V_FIRST:V_FIRST + V_SECOND]:
            fillers.append(lambda x=x: E_widen(*x))
        fillers.append(lambda: op("V", [], ("wp", 1), lambda: permute(wp, wl, 1)))
        for x in v_e[V_FIRST + V_SECOND:]:
            fillers.append(lambda x=x: E_widen(*x))
        for e in (0, 1):
            fillers.append(lambda e=e: V_ei(e, 0, 256))
            fillers.append(lambda e=e: V_ei(e, 256, 512))
        for e in (0, 1):
            fillers.append(lambda e=e: V_eq(e))
        for e in (2, 3):
            fillers.append(lambda e=e: V_ei(e, 0, 256))
            fillers.append(lambda e=e: V_ei(e, 256, 512))
            fillers.append(lambda e=e: V_eq(e))
        fill(V_FILL0)
        pend1, pend2 = [], []
        for k in range(0, n_units, 2):
            for c2 in range(1, len(CHUNKS)):
                if k == VZ_AT[c2]:
                    if Z_ENG[c2] == "V":
                        for j in chunk_j(c2):
                            Z_copy(c2, j, "V")
                    V_zq(c2)
            c, g, t = units[k]
            w = CHUNKS[c][1]
            for r in range(1, 4):
                for kk in (k, k + 1):
                    if not (kk in DOUBLE and r == 1):
                        V_fma(kk, r)
                if r == 1:
                    for f in pend1:
                        f()
                if r == 2:
                    for f in pend2:
                        f()
                fill(V_FILL[k // 2])
            pend1, pend2 = [], []
            if t == 2:
                last = k == n_units - 2
                hw = w // 2
                pend1 = [lambda c=c, g=g, hw=hw: V_ui(c, g, 0, hw), lambda c=c, g=g, w=w, hw=hw: V_ui(c, g, hw, w)]
                if last:
                    pend2 = [lambda c=c, g=g, hw=hw: V_uq(c, g, 0, hw), lambda c=c, g=g, w=w, hw=hw: V_uq(c, g, hw, w)]
                else:
                    pend2 = [lambda c=c, g=g, w=w: V_uq(c, g, 0, w)]
        for f in pend1 + pend2:
            f()
        assert not fillers
        for j in chunk_j(L):
            O_copy(L, j, 0, "V", "half")
            O_copy(L, j, 1, "S", "half")

        pos = {e: 0 for e in lists}
        left = sum(len(v) for v in lists.values())
        while left:
            moved = False
            for e in ("P", "S", "V", "G"):
                if pos[e] < len(lists[e]):
                    needs, gives, fn = lists[e][pos[e]]
                    if all(n in done for n in needs):
                        fn()
                        done.add(gives)
                        pos[e] += 1
                        left -= 1
                        moved = True
            assert moved, [lists[e][pos[e]][:2] for e in lists if pos[e] < len(lists[e])]
